import numpy as np
import ml_dtypes


def mxq(x, axis, fmt="e4m3"):
    dtype, down = {"e4m3": (ml_dtypes.float8_e4m3fn, 7), "e5m2": (ml_dtypes.float8_e5m2, 14)}[fmt]
    v = np.moveaxis(np.asarray(x, np.float32).astype(ml_dtypes.bfloat16).astype(np.float64), axis, -1)
    blocks = v.reshape(v.shape[:-1] + (-1, 32))
    amax = np.abs(blocks).max(-1, keepdims=True)
    byte = np.maximum(np.where(amax > 0, np.frexp(amax)[1] - 1 + 127, 0) - down, 1)
    scale = np.exp2(byte - 127.0)
    codes = (blocks / scale).astype(np.float32).astype(dtype).astype(np.float64)
    return np.moveaxis((codes * scale).reshape(v.shape), -1, axis)


WIDE = False


def mx_kscale(k):
    if not WIDE:
        return np.ones(k)
    levels = np.array([10, -10, 5, -5, 0])
    if k % 512:
        return np.exp2(np.random.permutation(np.resize(levels, k // 32))).repeat(32)
    a = np.empty((k // 512, 16))
    for p in range(k // 512):
        a[p, :8] = np.random.permutation(np.resize(levels, 8))
        for g in range(8):
            far = levels[np.abs(levels - a[p, g]) >= 10]
            a[p, g + 8] = far[np.random.randint(len(far))]
    return np.exp2(a.ravel()).repeat(32)


def f64(x):
    return np.asarray(x).astype(np.float64)


def striped(idx):
    return np.tile(idx.reshape(-1, 16).T, (8, 1)).astype(np.uint16)


def unstriped(offs):
    return offs[:16].T.reshape(-1).astype(np.int64)


E2M1 = np.array([0.0, 0.5, 1.0, 1.5, 2.0, 3.0, 4.0, 6.0, -0.0, -0.5, -1.0, -1.5, -2.0, -3.0, -4.0, -6.0])


def pack_weight(w, fmt):
    k, n = w.shape
    w = f64(np.asarray(w, np.float32).astype(ml_dtypes.bfloat16)).reshape(k // 32, 32, n)
    amax = np.abs(w).max(1)
    if fmt == "e4m3":
        byte = np.frexp(amax)[1] - 1 + 127 - 7
    else:
        mant, ex = np.frexp(amax / 6.0)
        byte = np.where(mant > 0.5, ex, ex - 1) + 127
    byte = np.clip(np.where(amax > 0, byte, 1), 1, 254)
    scaled = (w * np.exp2(127.0 - byte)[:, None, :]).reshape(k, n).astype(np.float32)
    by_word = np.ascontiguousarray(scaled.reshape(k // 512, 128, 4, n).transpose(0, 1, 3, 2))
    if fmt == "e4m3":
        words = by_word.astype(ml_dtypes.float8_e4m3fn).view(np.uint8)
    else:
        c = by_word.astype(ml_dtypes.float4_e2m1fn).view(np.uint8) & 0xF
        words = (c[..., 0::2] | (c[..., 1::2] << 4)).reshape(k // 512, 128, 2 * n)
    return np.ascontiguousarray(words), np.ascontiguousarray(byte.astype(np.uint8).reshape(k // 512, 16, n))


def unpack_weight(words, scales, fmt):
    g, _, n = scales.shape
    words = np.ascontiguousarray(words).reshape(g, 128, n, -1)
    if fmt == "e4m3":
        vals = words.view(ml_dtypes.float8_e4m3fn).astype(np.float64)
    else:
        nib = np.empty((g, 128, n, 4), np.uint8)
        nib[..., 0::2] = words & 0xF
        nib[..., 1::2] = words >> 4
        vals = E2M1[nib]
    vals = vals * np.repeat(np.exp2(scales.astype(np.float64) - 127.0), 8, axis=1)[..., None]
    return vals.transpose(0, 1, 3, 2).reshape(g * 512, n)


def gelu(v):
    return 0.5 * v * (1.0 + np.tanh(np.sqrt(2.0 / np.pi) * (v + 0.044715 * v**3)))


K, T, S, H, T3, S2, P = 512, 2048, 1024, 1536, 2048, 512, 512

def setup_inputs():
    n = np.random.standard_normal
    s = mx_kscale(K)[:, None]
    u = mx_kscale(H)[:, None]
    d = {}
    d["tab_words"], d["tab_scales"] = pack_weight(n((K, T)) * s, "e4m3")
    d["tab2_words"], d["tab2_scales"] = pack_weight(n((H, T3)) / H ** 0.5 / u, "e4m3")
    d["w1"] = (1.5 * n((K, H)) / K ** 0.5 / s).astype(np.float32)
    d["w4_words"], d["w4_scales"] = pack_weight(2.0 * n((K, H)) / K ** 0.5 / s * u.T, "e2m1")
    d["ref"] = (0.8 * n((S2, P))).astype(np.float32)
    d["offs"] = striped(np.random.permutation(T)[:S])
    d["offs2"] = striped(np.random.permutation(T3)[:S2])
    d["pos1"] = striped(np.random.permutation(S)[:P])
    d["pos2"] = striped(np.random.permutation(S)[:P])
    return d

def reference(tab_words, tab_scales, tab2_words, tab2_scales, w1, w4_words, w4_scales, ref, offs, offs2, pos1, pos2):
    v = unpack_weight(tab_words, tab_scales, "e4m3")[:, unstriped(offs)]
    v2 = unpack_weight(tab2_words, tab2_scales, "e4m3")[:, unstriped(offs2)]
    w4 = unpack_weight(w4_words, w4_scales, "e2m1")
    a = mxq(f64(w1), 0, "e4m3").T @ v
    b = w4.T @ v
    damp = 1.0 / (1.0 + np.abs(a))
    h = b * damp
    e = v2.T @ mxq(h, 0, "e4m3")
    x = e[:, unstriped(pos1)] - f64(ref)
    before = 0.5 * x * (1.0 + np.tanh(0.7978845608 * (x + 0.044715 * x ** 3)))
    out = before + e[:, unstriped(pos2)]
    return out

@@ -1,0 +1,331 @@
+from contextlib import ExitStack
+
+import concourse.mybir as mybir
+
+F32 = mybir.dt.float32
+BF16 = mybir.dt.bfloat16
+I32 = mybir.dt.int32
+U32 = mybir.dt.uint32
+U16 = mybir.dt.uint16
+U8 = mybir.dt.uint8
+E4M3 = mybir.dt.float8_e4m3fn_x4
+E2M1 = mybir.dt.float4_e2m1fn_x4
+ALU = mybir.AluOpType
+ACT = mybir.ActivationFunctionType
+
+K, T, S, H, T2, S2, PAIRS = 512, 2048, 1024, 1536, 2048, 512, 512
+P = 128
+PACK = 4
+PASS = P * PACK
+GROUPS = H // PASS
+JW = 128
+UNITS_PER_GROUP = S // JW
+UNITS = GROUPS * UNITS_PER_GROUP
+VW = 256
+M_TILES = S2 // P
+
+FLOPS = 2 * 2 * K * H * S + 2 * H * S2 * S
+
+SQ = "SVGGGGGGGGGGGGGGGGGGGGVS"
+CAST = "SV,S,S"
+ECOPY = "VVVVVV"
+FINE = (0, 11)
+DAMP_TAG = "damp"
+H_TAG = "h"
+RING = 3
+WARM = True
+
+
+def tile_list_breath_pattern_response_kernel(
+    tc, tab_words, tab_scales, tab2_words, tab2_scales, w1, w4_words, w4_scales, ref, offs, offs2, pos1, pos2, out
+):
+    nc = tc.nc
+    with ExitStack() as ctx:
+        held = ctx.enter_context(tc.tile_pool(name="held", bufs=1))
+        work = ctx.enter_context(tc.tile_pool(name="work", bufs=4))
+        psum = ctx.enter_context(tc.psum_pool(name="psum", bufs=1))
+
+        def keep(name, shape, dtype):
+            return held.tile(shape, dtype, name=name, align_bytes=64)
+
+        offs_t = keep("offs_t", [P, S // 16], U16)
+        offs2_t = keep("offs2_t", [P, S2 // 16], U16)
+        pos1_t = keep("pos1_t", [P, PAIRS // 16], U16)
+        pos2_t = keep("pos2_t", [P, PAIRS // 16], U16)
+        tab_w = keep("tab_w", [P, T], I32)
+        tab_s = keep("tab_s", [P, T], U8)
+        tab2_w = [keep("tab2_w%d" % g, [P, T2], I32) for g in range(GROUPS)]
+        tab2_s = keep("tab2_s", [P, T2], U8)
+        w1_raw = [keep("w1_raw%d" % g, [P, PACK, PASS], F32) for g in range(GROUPS)]
+        w4_raw = [keep("w4_raw%d" % g, [P, 2 * PASS], U8) for g in range(GROUPS)]
+        w4_sraw = keep("w4_sraw", [P, H], U8)
+        ref_t = keep("ref_t", [P, M_TILES, PAIRS], F32)
+
+        def load_w1(g, eng):
+            eng.dma_start(w1_raw[g][:], w1[:, g * PASS : (g + 1) * PASS].rearrange("(p i) c -> p i c", i=PACK))
+
+        def load_w4(g):
+            nc.sync.dma_start(w4_raw[g][:].bitcast(I32), w4_words[0, :, 2 * g * PASS : 2 * (g + 1) * PASS].bitcast(I32))
+
+        def load_plane(eng, plane, rows):
+            words = rows.shape[1] // 4
+            for quad in range(4):
+                src = rows[4 * quad : 4 * quad + 4, :].bitcast(I32).unsqueeze(0).to_broadcast([8, 4, words])
+                eng.dma_start(plane[32 * quad : 32 * quad + 32, :].bitcast(I32), src)
+
+        load_w1(0, nc.sync)
+        if WARM:
+            warm_in = keep("warm_in", [P, 1], F32)
+            warm_out = keep("warm_out", [P, 1], F32)
+            nc.vector.memset(warm_in[:], 1.0)
+            nc.scalar.activation(warm_out[:], warm_in[:], ACT.Abs_reciprocal_sqrt)
+        nc.sync.dma_start(offs_t[:], offs)
+        load_plane(nc.sync, tab_s, tab_scales[0])
+        nc.sync.dma_start(tab_w[:], tab_words[0].rearrange("p t i -> p (t i)").bitcast(I32))
+        load_w4(0)
+        load_plane(nc.sync, w4_sraw, w4_scales[0])
+        nc.gpsimd.memset(tab2_s[:].bitcast(I32), 0)
+        for g in range(1, GROUPS):
+            load_w1(g, nc.sync)
+            load_w4(g)
+        nc.sync.dma_start(offs2_t[:], offs2)
+        for quad in range(4):
+            nc.sync.dma_start(
+                tab2_s[32 * quad : 32 * quad + 4 * GROUPS, :].bitcast(I32),
+                tab2_scales[:, 4 * quad : 4 * quad + 4, :].bitcast(I32),
+            )
+        for g in range(GROUPS):
+            nc.sync.dma_start(tab2_w[g][:], tab2_words[g].rearrange("p t i -> p (t i)").bitcast(I32))
+        nc.sync.dma_start(ref_t[:], ref.rearrange("(c p) j -> p c j", p=P))
+        nc.sync.dma_start(pos1_t[:], pos1)
+        nc.sync.dma_start(pos2_t[:], pos2)
+
+        v_w = [keep("v_w%d" % c, [P, VW], U32) for c in range(S // VW)]
+        v_s = [keep("v_s%d" % c, [P, VW], U8) for c in range(S // VW)]
+        v2_w = [keep("v2_w%d" % g, [P, S2], U32) for g in range(GROUPS)]
+        v2_s = keep("v2_s", [P, S2], U8)
+        w1_bf = [keep("w1_bf%d" % g, [P, PACK * PASS], BF16) for g in range(GROUPS)]
+        w1_w = [keep("w1_w%d" % g, [P, PASS], U32) for g in range(GROUPS)]
+        w1_s = [keep("w1_s%d" % g, [P, PASS], U8) for g in range(GROUPS)]
+        w4_w = [keep("w4_w%d" % g, [P, 2 * PASS], U8) for g in range(GROUPS)]
+        w4_s = [keep("w4_s%d" % g, [P, PASS], U8) for g in range(GROUPS)]
+        h_w = [[keep("h_w%d_%d" % (g, c), [P, VW], U32) for c in range(S // VW)] for g in range(GROUPS)]
+        h_s = [[keep("h_s%d_%d" % (g, c), [P, VW], U8) for c in range(S // VW)] for g in range(GROUPS)]
+        e_t = [keep("e_t%d" % m, [P, S], F32) for m in range(M_TILES)]
+
+        def gather_v_words(c):
+            nc.vector.tensor_copy(v_w[c][:], tab_w[:].bitcast(U32).indirect(offs_t[:, c * VW // 16 : (c + 1) * VW // 16]))
+
+        def gather_v_scales(c):
+            nc.vector.tensor_copy(v_s[c][:], tab_s[:].indirect(offs_t[:, c * VW // 16 : (c + 1) * VW // 16]))
+
+        def gather_v2_words(g):
+            nc.vector.tensor_copy(v2_w[g][:], tab2_w[g][:].bitcast(U32).indirect(offs2_t[:]))
+
+        def gather_v2_scales():
+            nc.vector.tensor_copy(v2_s[:], tab2_s[:].indirect(offs2_t[:]))
+
+        def cast_w1(g):
+            dst_all = w1_bf[g][:].rearrange("p (t q i) -> p q i t", t=PACK, i=PACK)
+            src_all = w1_raw[g][:].rearrange("p i (q t) -> p q i t", t=PACK)
+            engines = CAST.split(",")[g]
+            share = P // len(engines)
+            for n, eng in enumerate(engines):
+                dst = dst_all[:, n * share : (n + 1) * share]
+                src = src_all[:, n * share : (n + 1) * share]
+                if eng == "S":
+                    nc.scalar.copy(dst, src)
+                elif eng == "V":
+                    nc.vector.tensor_copy(dst, src)
+                else:
+                    nc.gpsimd.tensor_scalar(dst, src, 1.0, 0.0, ALU.mult, ALU.add)
+
+        def quantise_w1(g):
+            nc.vector.quantize_mx(w1_w[g][:].bitcast(E4M3), w1_s[g][:], w1_bf[g][:])
+
+        def deal_w4_words(g):
+            nc.vector.tensor_copy(
+                w4_w[g][:].bitcast(U16).rearrange("p (t o i) -> p o t i", t=PACK, i=8),
+                w4_raw[g][:].bitcast(U16).rearrange("p (o i t) -> p o t i", t=PACK, i=8),
+            )
+
+        def deal_w4_scales(g):
+            nc.vector.tensor_copy(
+                w4_s[g][:].rearrange("p (t o i) -> p o t i", t=PACK, i=16),
+                w4_sraw[:, g * PASS : (g + 1) * PASS].rearrange("p (o i t) -> p o t i", t=PACK, i=16),
+            )
+
+        state = {}
+
+        def place(u):
+            g, jc = divmod(u, UNITS_PER_GROUP)
+            c, half = divmod(jc, VW // JW)
+            return g, c, slice(half * JW, (half + 1) * JW)
+
+        def product_a(u):
+            g, c, cols = place(u)
+            bank = psum.tile([P, PACK, JW], F32, name="a_bank", bufs=3)
+            for t in range(PACK):
+                rows = slice(t * P, (t + 1) * P)
+                nc.tensor.matmul_mx(
+                    bank[:, t, :], lhsT=w1_w[g][:, rows].bitcast(E4M3), lhsT_scale=w1_s[g][:, rows],
+                    rhs=v_w[c][:, cols].bitcast(E4M3), rhs_scale=v_s[c][:, cols], start=True, stop=True,
+                )
+            state["a", u] = bank
+
+        def product_b(u):
+            g, c, cols = place(u)
+            bank = psum.tile([P, PACK, JW], F32, name="b_bank", bufs=3)
+            for t in range(PACK):
+                nc.tensor.matmul_mx(
+                    bank[:, t, :], lhsT=w4_w[g][:, 2 * t * P : 2 * (t + 1) * P].bitcast(E2M1),
+                    lhsT_scale=w4_s[g][:, t * P : (t + 1) * P],
+                    rhs=v_w[c][:, cols].bitcast(E4M3), rhs_scale=v_s[c][:, cols], start=True, stop=True,
+                )
+            state["b", u] = bank
+
+        def halves(pair):
+            return (2 * pair, 2 * pair + 1)
+
+        def part(tile, u):
+            return tile[:, (u % 2) * JW : (u % 2 + 1) * JW, :]
+
+        def pair_tile(kind, u, dtype, tag, bufs):
+            if u % 2 == 0:
+                state[kind, u // 2] = work.tile([P, VW, PACK], dtype, name=kind, tag=tag, bufs=bufs, align_bytes=64)
+            return state[kind, u // 2]
+
+        def absolute(u):
+            size = pair_tile("size", u, F32, "size", 3)
+            nc.scalar.activation(part(size, u), state["a", u][:].rearrange("p t j -> p j t"), ACT.Abs)
+
+        def root(u):
+            r = pair_tile("root", u, F32, "root", 3)
+            size = state["size", u // 2]
+            if u // 2 in FINE:
+                nc.scalar.activation(part(r, u), part(size, u), ACT.Abs_reciprocal_sqrt, bias=1.0)
+            elif u % 2 == 1:
+                nc.scalar.activation(r[:], size[:], ACT.Abs_reciprocal_sqrt, bias=1.0)
+
+        def square(u):
+            damp = pair_tile("damp", u, F32, DAMP_TAG, RING)
+            r = state["root", u // 2]
+            if u % 2 == 0 and SQ[u] == SQ[u + 1] and SQ[u] != "G" and u // 2 not in FINE:
+                dst, src = damp[:], r[:]
+            elif u % 2 == 1 and SQ[u] == SQ[u - 1] and SQ[u] != "G" and u // 2 not in FINE:
+                return
+            else:
+                dst, src = part(damp, u), part(r, u)
+            if SQ[u] == "S":
+                nc.scalar.activation(dst, src, ACT.Square)
+            elif SQ[u] == "V":
+                nc.vector.tensor_tensor(dst, src, src, ALU.mult)
+            else:
+                nc.gpsimd.tensor_tensor(dst, src, src, ALU.mult)
+
+        def damped(u):
+            h = pair_tile("h", u, BF16, H_TAG, RING)
+            nc.vector.tensor_tensor(
+                part(h, u), state["b", u][:].rearrange("p t j -> p j t"), part(state["damp", u // 2], u), ALU.mult
+            )
+
+        def quantise_h(u):
+            g, c, cols = place(u)
+            h = state["h", u // 2]
+            if u // 2 in FINE:
+                nc.vector.quantize_mx(
+                    h_w[g][c][:, cols].bitcast(E4M3), h_s[g][c][:, cols], part(h, u).rearrange("p j t -> p (j t)")
+                )
+            elif u % 2 == 1:
+                nc.vector.quantize_mx(h_w[g][c][:].bitcast(E4M3), h_s[g][c][:], h[:].rearrange("p j t -> p (j t)"))
+
+        def score_pass(dst, m, g, c, cols):
+            nc.tensor.matmul_mx(
+                dst, lhsT=v2_w[g][:, m * P : (m + 1) * P].bitcast(E4M3),
+                lhsT_scale=v2_s[4 * g : P, m * P : (m + 1) * P],
+                rhs=h_w[g][c][:, cols].bitcast(E4M3), rhs_scale=h_s[g][c][:, cols],
+                start=(g == 0), stop=(g == GROUPS - 1),
+            )
+
+        def copy_scores(eng, m, first, src):
+            dst = e_t[m][:, first : first + src.shape[1]]
+            if eng == "S":
+                nc.scalar.copy(dst, src)
+            else:
+                nc.vector.tensor_copy(dst, src)
+
+        def scores(u):
+            g, c, cols = place(u)
+            if g < GROUPS - 1:
+                return
+            if u == UNITS - 1:
+                banks = [psum.tile([P, PACK, JW], F32, name="a_bank", bufs=3) for m in range(M_TILES - 1)]
+                banks.append(psum.tile([P, PACK, JW], F32, name="e_bank", bufs=2))
+                for gg in range(GROUPS):
+                    for m in range(M_TILES):
+                        score_pass(banks[m][:, 0, :], m, gg, c, cols)
+                for m in range(M_TILES):
+                    copy_scores("S", m, c * VW + cols.start, banks[m][:, 0, :])
+            elif u == UNITS - 2:
+                bank = psum.tile([P, PACK, JW], F32, name="e_bank", bufs=2)
+                for m in range(M_TILES):
+                    for gg in range(GROUPS):
+                        score_pass(bank[:, m, :], m, gg, c, cols)
+                for m in range(M_TILES):
+                    copy_scores("S", m, c * VW + cols.start, bank[:, m, :])
+            elif u % 2 == 1:
+                for mm in range(M_TILES // 2):
+                    bank = psum.tile([P, 2, VW], F32, name="e_bank", bufs=2)
+                    for i in range(2):
+                        for gg in range(GROUPS):
+                            score_pass(bank[:, i, :], 2 * mm + i, gg, c, slice(0, VW))
+                    for i in range(2):
+                        copy_scores(ECOPY[2 * c + mm], 2 * mm + i, c * VW, bank[:, i, :])
+
+        cast_w1(0)
+        gather_v_scales(0)
+        quantise_w1(0)
+        gather_v_words(0)
+        deal_w4_words(0)
+        deal_w4_scales(0)
+
+        side = {
+            0: [lambda: gather_v_words(1), lambda: gather_v_scales(1)],
+            1: [lambda: gather_v_words(2), lambda: gather_v_scales(2)],
+            2: [lambda: cast_w1(1)],
+            3: [lambda: gather_v_words(3), lambda: gather_v_scales(3)],
+            5: [lambda: quantise_w1(1), lambda: deal_w4_words(1), lambda: deal_w4_scales(1)],
+            9: [lambda: cast_w1(2)],
+            10: [lambda: deal_w4_words(2), lambda: deal_w4_scales(2)],
+            12: [lambda: quantise_w1(2), gather_v2_scales],
+            13: [lambda: gather_v2_words(0)],
+            15: [lambda: gather_v2_words(1)],
+            17: [lambda: gather_v2_words(2)],
+        }
+        stages = [(0, product_a), (1, absolute), (2, root), (4, square), (5, product_b), (6, damped), (7, quantise_h), (7, scores)]
+        for step in range(UNITS + 7):
+            for lag, stage in stages:
+                if 0 <= step - lag < UNITS:
+                    stage(step - lag)
+            for job in side.get(step - 1, []):
+                job()
+
+        def less_ref(m):
+            x = work.tile([P, PAIRS], F32, name="x")
+            nc.vector.tensor_tensor(x[:], e_t[m][:].indirect(pos1_t[:]), ref_t[:, m, :], ALU.subtract)
+            state["x", m] = x
+
+        def finish(m):
+            before = work.tile([P, PAIRS], F32, name="before")
+            nc.scalar.activation(before[:], state["x", m][:], ACT.Gelu_apprx_tanh)
+            res = work.tile([P, PAIRS], F32, name="res")
+            nc.vector.tensor_tensor(res[:], e_t[m][:].indirect(pos2_t[:]), before[:], ALU.add)
+            nc.sync.dma_start(out[m * P : (m + 1) * P, :], res[:])
+
+        ahead = 2
+        for m in range(ahead):
+            less_ref(m)
+        for m in range(M_TILES):
+            if m + ahead < M_TILES:
+                less_ref(m + ahead)
+            finish(m)

@@ -26,9 +26,9 @@ M_TILES = S2 // P
 
 FLOPS = 2 * 2 * K * H * S + 2 * H * S2 * S
 
-SQ = "SVGGGGGGGGGGGGGGGGGGGGVS"
-CAST = "SV,S,S"
-ECOPY = "VVVVVV"
+SQ = "SSVVSSVVSSVVSSSSSSSSVVSS"
+CAST = "SV,V,V"
+ECOPY = "VSVSVS"
 FINE = (0, 11)
 DAMP_TAG = "damp"
 H_TAG = "h"
@@ -73,7 +73,6 @@ def tile_list_breath_pattern_response_kernel(
                 src = rows[4 * quad : 4 * quad + 4, :].bitcast(I32).unsqueeze(0).to_broadcast([8, 4, words])
                 eng.dma_start(plane[32 * quad : 32 * quad + 32, :].bitcast(I32), src)
 
-        load_w1(0, nc.sync)
         if WARM:
             warm_in = keep("warm_in", [P, 1], F32)
             warm_out = keep("warm_out", [P, 1], F32)
@@ -81,6 +80,7 @@ def tile_list_breath_pattern_response_kernel(
             nc.scalar.activation(warm_out[:], warm_in[:], ACT.Abs_reciprocal_sqrt)
         nc.sync.dma_start(offs_t[:], offs)
         load_plane(nc.sync, tab_s, tab_scales[0])
+        load_w1(0, nc.sync)
         nc.sync.dma_start(tab_w[:], tab_words[0].rearrange("p t i -> p (t i)").bitcast(I32))
         load_w4(0)
         load_plane(nc.sync, w4_sraw, w4_scales[0])
@@ -100,8 +100,11 @@ def tile_list_breath_pattern_response_kernel(
         nc.sync.dma_start(pos1_t[:], pos1)
         nc.sync.dma_start(pos2_t[:], pos2)
 
-        v_w = [keep("v_w%d" % c, [P, VW], U32) for c in range(S // VW)]
-        v_s = [keep("v_s%d" % c, [P, VW], U8) for c in range(S // VW)]
+        v_w_first = keep("v_w_first", [P, VW], U32)
+        v_w_rest = keep("v_w_rest", [P, S - VW], U32)
+        v_w = [v_w_first[:]] + [v_w_rest[:, c * VW : (c + 1) * VW] for c in range(S // VW - 1)]
+        v_s_all = keep("v_s_all", [P, S], U8)
+        v_s = [v_s_all[:, c * VW : (c + 1) * VW] for c in range(S // VW)]
         v2_w = [keep("v2_w%d" % g, [P, S2], U32) for g in range(GROUPS)]
         v2_s = keep("v2_s", [P, S2], U8)
         w1_bf = [keep("w1_bf%d" % g, [P, PACK * PASS], BF16) for g in range(GROUPS)]
@@ -109,15 +112,18 @@ def tile_list_breath_pattern_response_kernel(
         w1_s = [keep("w1_s%d" % g, [P, PASS], U8) for g in range(GROUPS)]
         w4_w = [keep("w4_w%d" % g, [P, 2 * PASS], U8) for g in range(GROUPS)]
         w4_s = [keep("w4_s%d" % g, [P, PASS], U8) for g in range(GROUPS)]
-        h_w = [[keep("h_w%d_%d" % (g, c), [P, VW], U32) for c in range(S // VW)] for g in range(GROUPS)]
-        h_s = [[keep("h_s%d_%d" % (g, c), [P, VW], U8) for c in range(S // VW)] for g in range(GROUPS)]
+        h_w_all = [keep("h_w%d" % g, [P, S], U32) for g in range(GROUPS)]
+        h_s_all = [keep("h_s%d" % g, [P, S], U8) for g in range(GROUPS)]
+        h_w = [[h_w_all[g][:, c * VW : (c + 1) * VW] for c in range(S // VW)] for g in range(GROUPS)]
+        h_s = [[h_s_all[g][:, c * VW : (c + 1) * VW] for c in range(S // VW)] for g in range(GROUPS)]
         e_t = [keep("e_t%d" % m, [P, S], F32) for m in range(M_TILES)]
 
-        def gather_v_words(c):
-            nc.vector.tensor_copy(v_w[c][:], tab_w[:].bitcast(U32).indirect(offs_t[:, c * VW // 16 : (c + 1) * VW // 16]))
+        def gather_v_words(first):
+            dst, cols = (v_w_first, slice(0, VW // 16)) if first else (v_w_rest, slice(VW // 16, S // 16))
+            nc.vector.tensor_copy(dst[:], tab_w[:].bitcast(U32).indirect(offs_t[:, cols]))
 
-        def gather_v_scales(c):
-            nc.vector.tensor_copy(v_s[c][:], tab_s[:].indirect(offs_t[:, c * VW // 16 : (c + 1) * VW // 16]))
+        def gather_v_scales():
+            nc.vector.tensor_copy(v_s_all[:], tab_s[:].indirect(offs_t[:]))
 
         def gather_v2_words(g):
             nc.vector.tensor_copy(v2_w[g][:], tab2_w[g][:].bitcast(U32).indirect(offs2_t[:]))
@@ -240,10 +246,11 @@ def tile_list_breath_pattern_response_kernel(
                 nc.vector.quantize_mx(h_w[g][c][:].bitcast(E4M3), h_s[g][c][:], h[:].rearrange("p j t -> p (j t)"))
 
         def score_pass(dst, m, g, c, cols):
+            cols = slice(c * VW + cols.start, c * VW + cols.stop)
             nc.tensor.matmul_mx(
                 dst, lhsT=v2_w[g][:, m * P : (m + 1) * P].bitcast(E4M3),
                 lhsT_scale=v2_s[4 * g : P, m * P : (m + 1) * P],
-                rhs=h_w[g][c][:, cols].bitcast(E4M3), rhs_scale=h_s[g][c][:, cols],
+                rhs=h_w_all[g][:, cols].bitcast(E4M3), rhs_scale=h_s_all[g][:, cols],
                 start=(g == 0), stop=(g == GROUPS - 1),
             )
 
@@ -273,7 +280,13 @@ def tile_list_breath_pattern_response_kernel(
                         score_pass(bank[:, m, :], m, gg, c, cols)
                 for m in range(M_TILES):
                     copy_scores("S", m, c * VW + cols.start, bank[:, m, :])
-            elif u % 2 == 1:
+            elif c == 1 and u % 2 == 1:
+                for m in range(M_TILES):
+                    bank = psum.tile([P, 2 * VW], F32, name="e_bank", bufs=2)
+                    for gg in range(GROUPS):
+                        score_pass(bank[:], m, gg, 0, slice(0, 2 * VW))
+                    copy_scores(ECOPY[m], m, 0, bank[:])
+            elif c == 2 and u % 2 == 1:
                 for mm in range(M_TILES // 2):
                     bank = psum.tile([P, 2, VW], F32, name="e_bank", bufs=2)
                     for i in range(2):
@@ -282,18 +295,16 @@ def tile_list_breath_pattern_response_kernel(
                     for i in range(2):
                         copy_scores(ECOPY[2 * c + mm], 2 * mm + i, c * VW, bank[:, i, :])
 
+        gather_v_scales()
         cast_w1(0)
-        gather_v_scales(0)
         quantise_w1(0)
-        gather_v_words(0)
+        gather_v_words(True)
         deal_w4_words(0)
         deal_w4_scales(0)
+        gather_v_words(False)
 
         side = {
-            0: [lambda: gather_v_words(1), lambda: gather_v_scales(1)],
-            1: [lambda: gather_v_words(2), lambda: gather_v_scales(2)],
             2: [lambda: cast_w1(1)],
-            3: [lambda: gather_v_words(3), lambda: gather_v_scales(3)],
             5: [lambda: quantise_w1(1), lambda: deal_w4_words(1), lambda: deal_w4_scales(1)],
             9: [lambda: cast_w1(2)],
             10: [lambda: deal_w4_words(2), lambda: deal_w4_scales(2)],
@@ -319,8 +330,13 @@ def tile_list_breath_pattern_response_kernel(
             before = work.tile([P, PAIRS], F32, name="before")
             nc.scalar.activation(before[:], state["x", m][:], ACT.Gelu_apprx_tanh)
             res = work.tile([P, PAIRS], F32, name="res")
-            nc.vector.tensor_tensor(res[:], e_t[m][:].indirect(pos2_t[:]), before[:], ALU.add)
-            nc.sync.dma_start(out[m * P : (m + 1) * P, :], res[:])
+            pieces = 2 if m == M_TILES - 1 else 1
+            width = PAIRS // pieces
+            for n in range(pieces):
+                cols = slice(n * width, (n + 1) * width)
+                picks = pos2_t[:, cols.start // 16 : cols.stop // 16]
+                nc.vector.tensor_tensor(res[:, cols], e_t[m][:].indirect(picks), before[:, cols], ALU.add)
+                nc.sync.dma_start(out[m * P : (m + 1) * P, cols], res[:, cols])
 
         ahead = 2
         for m in range(ahead):

@@ -26,13 +26,14 @@ M_TILES = S2 // P
 
 FLOPS = 2 * 2 * K * H * S + 2 * H * S2 * S
 
-SQ = "SSVVSSVVSSVVSSSSSSSSVVSS"
+SQ = "SGSGSGSGSGSGSGSGSGSGSGVS"
 CAST = "SV,V,V"
-ECOPY = "VSVSVS"
+ECOPY = "VVVVVV"
 FINE = (0, 11)
 DAMP_TAG = "damp"
 H_TAG = "h"
 RING = 3
+ORDER = [(0, c) for c in range(S // VW)] + [(g, c) for c in range(S // VW) for g in range(1, GROUPS)]
 WARM = True
 
 
@@ -164,8 +165,8 @@ def tile_list_breath_pattern_response_kernel(
         state = {}
 
         def place(u):
-            g, jc = divmod(u, UNITS_PER_GROUP)
-            c, half = divmod(jc, VW // JW)
+            pair, half = divmod(u, VW // JW)
+            g, c = ORDER[pair]
             return g, c, slice(half * JW, (half + 1) * JW)
 
         def product_a(u):
@@ -214,26 +215,19 @@ def tile_list_breath_pattern_response_kernel(
                 nc.scalar.activation(r[:], size[:], ACT.Abs_reciprocal_sqrt, bias=1.0)
 
         def square(u):
-            damp = pair_tile("damp", u, F32, DAMP_TAG, RING)
-            r = state["root", u // 2]
-            if u % 2 == 0 and SQ[u] == SQ[u + 1] and SQ[u] != "G" and u // 2 not in FINE:
-                dst, src = damp[:], r[:]
-            elif u % 2 == 1 and SQ[u] == SQ[u - 1] and SQ[u] != "G" and u // 2 not in FINE:
-                return
-            else:
-                dst, src = part(damp, u), part(r, u)
+            damp = work.tile([P, JW, PACK], F32, name="damp", tag="ring" if u % 2 else "damp", bufs=3, align_bytes=64)
+            src = part(state["root", u // 2], u)
             if SQ[u] == "S":
-                nc.scalar.activation(dst, src, ACT.Square)
+                nc.scalar.activation(damp[:], src, ACT.Square)
             elif SQ[u] == "V":
-                nc.vector.tensor_tensor(dst, src, src, ALU.mult)
+                nc.vector.tensor_tensor(damp[:], src, src, ALU.mult)
             else:
-                nc.gpsimd.tensor_tensor(dst, src, src, ALU.mult)
+                nc.gpsimd.tensor_tensor(damp[:], src, src, ALU.mult)
+            state["damp", u] = damp
 
         def damped(u):
-            h = pair_tile("h", u, BF16, H_TAG, RING)
-            nc.vector.tensor_tensor(
-                part(h, u), state["b", u][:].rearrange("p t j -> p j t"), part(state["damp", u // 2], u), ALU.mult
-            )
+            h = pair_tile("h", u, BF16, "ring", 3)
+            nc.vector.tensor_tensor(part(h, u), state["b", u][:].rearrange("p t j -> p j t"), state["damp", u][:], ALU.mult)
 
         def quantise_h(u):
             g, c, cols = place(u)
@@ -245,13 +239,13 @@ def tile_list_breath_pattern_response_kernel(
             elif u % 2 == 1:
                 nc.vector.quantize_mx(h_w[g][c][:].bitcast(E4M3), h_s[g][c][:], h[:].rearrange("p j t -> p (j t)"))
 
-        def score_pass(dst, m, g, c, cols):
+        def score_pass(dst, m, g, c, cols, may_stop=True):
             cols = slice(c * VW + cols.start, c * VW + cols.stop)
             nc.tensor.matmul_mx(
                 dst, lhsT=v2_w[g][:, m * P : (m + 1) * P].bitcast(E4M3),
                 lhsT_scale=v2_s[4 * g : P, m * P : (m + 1) * P],
                 rhs=h_w_all[g][:, cols].bitcast(E4M3), rhs_scale=h_s_all[g][:, cols],
-                start=(g == 0), stop=(g == GROUPS - 1),
+                start=(g == 0), stop=(g == GROUPS - 1 and may_stop),
             )
 
         def copy_scores(eng, m, first, src):
@@ -263,23 +257,21 @@ def tile_list_breath_pattern_response_kernel(
 
         def scores(u):
             g, c, cols = place(u)
+            if u == UNITS - 3:
+                banks = [psum.tile([P, VW], F32, name="e_bank", bufs=2) for m in range(2)]
+                banks = banks + [psum.tile([P, VW], F32, name="a_bank", bufs=3) for m in range(2)]
+                state["last"] = banks
+                for gg in range(GROUPS - 1):
+                    for m in range(M_TILES):
+                        score_pass(banks[m][:], m, gg, c, slice(0, VW), False)
             if g < GROUPS - 1:
                 return
-            if u == UNITS - 1:
-                banks = [psum.tile([P, PACK, JW], F32, name="a_bank", bufs=3) for m in range(M_TILES - 1)]
-                banks.append(psum.tile([P, PACK, JW], F32, name="e_bank", bufs=2))
-                for gg in range(GROUPS):
+            if u >= UNITS - 2:
+                for m in range(M_TILES):
+                    score_pass(state["last"][m][:, cols], m, g, c, cols, u == UNITS - 1)
+                if u == UNITS - 1:
                     for m in range(M_TILES):
-                        score_pass(banks[m][:, 0, :], m, gg, c, cols)
-                for m in range(M_TILES):
-                    copy_scores("S", m, c * VW + cols.start, banks[m][:, 0, :])
-            elif u == UNITS - 2:
-                bank = psum.tile([P, PACK, JW], F32, name="e_bank", bufs=2)
-                for m in range(M_TILES):
-                    for gg in range(GROUPS):
-                        score_pass(bank[:, m, :], m, gg, c, cols)
-                for m in range(M_TILES):
-                    copy_scores("S", m, c * VW + cols.start, bank[:, m, :])
+                        copy_scores("S", m, c * VW, state["last"][m][:])
             elif c == 1 and u % 2 == 1:
                 for m in range(M_TILES):
                     bank = psum.tile([P, 2 * VW], F32, name="e_bank", bufs=2)
@@ -304,11 +296,11 @@ def tile_list_breath_pattern_response_kernel(
         gather_v_words(False)
 
         side = {
-            2: [lambda: cast_w1(1)],
-            5: [lambda: quantise_w1(1), lambda: deal_w4_words(1), lambda: deal_w4_scales(1)],
-            9: [lambda: cast_w1(2)],
-            10: [lambda: deal_w4_words(2), lambda: deal_w4_scales(2)],
-            12: [lambda: quantise_w1(2), gather_v2_scales],
+            1: [lambda: cast_w1(1)],
+            3: [lambda: quantise_w1(1), lambda: deal_w4_words(1), lambda: deal_w4_scales(1)],
+            5: [lambda: cast_w1(2)],
+            7: [lambda: quantise_w1(2), lambda: deal_w4_words(2), lambda: deal_w4_scales(2)],
+            11: [gather_v2_scales],
             13: [lambda: gather_v2_words(0)],
             15: [lambda: gather_v2_words(1)],
             17: [lambda: gather_v2_words(2)],

@@ -13,28 +13,34 @@ E2M1 = mybir.dt.float4_e2m1fn_x4
 ALU = mybir.AluOpType
 ACT = mybir.ActivationFunctionType
 
-K, T, S, H, T2, S2, PAIRS = 512, 2048, 1024, 1536, 2048, 512, 512
+K, T, S, H, T2, S2, OUT_COLS = 512, 2048, 1024, 1536, 2048, 512, 512
+FLOPS = 2 * 2 * K * H * S + 2 * H * S2 * S
+
 P = 128
 PACK = 4
 PASS = P * PACK
+LIST_COL = 16
 GROUPS = H // PASS
-JW = 128
-UNITS_PER_GROUP = S // JW
-UNITS = GROUPS * UNITS_PER_GROUP
-VW = 256
+UNIT_W = 128
+PAIR_W = 2 * UNIT_W
+CHUNKS = S // PAIR_W
 M_TILES = S2 // P
 
-FLOPS = 2 * 2 * K * H * S + 2 * H * S2 * S
+PAIR_ORDER = [(0, c) for c in range(CHUNKS)] + [(g, c) for c in range(CHUNKS) for g in range(1, GROUPS)]
+PAIRS = len(PAIR_ORDER)
+UNITS = 2 * PAIRS
+END_PAIRS = (0, PAIRS - 1)
 
-SQ = "SGSGSGSGSGSGSGSGSGSGSGVS"
-CAST = "SV,V,V"
-ECOPY = "VVVVVV"
-FINE = (0, 11)
-DAMP_TAG = "damp"
-H_TAG = "h"
-RING = 3
-ORDER = [(0, c) for c in range(S // VW)] + [(g, c) for c in range(S // VW) for g in range(1, GROUPS)]
-WARM = True
+CHAIN = 5
+CHAINED_H = PAIRS - 3
+CAST_AFTER = 1
+V2_AFTER = 3
+HELD_ROOTS = (CAST_AFTER,) + tuple(range(V2_AFTER, V2_AFTER + GROUPS + 1))
+
+A_BANKS, B_BANKS, E_BANKS = 3, 3, 2
+ROOT_BUFS = 3
+DAMP_BUFS = 4
+ABS_LAG, ROOT_LAG, SQUARE_LAG, B_LAG, DAMPED_LAG, QUANTISE_LAG = 1, 2, 4, 5, 6, 7
 
 
 def tile_list_breath_pattern_response_kernel(
@@ -43,52 +49,53 @@ def tile_list_breath_pattern_response_kernel(
     nc = tc.nc
     with ExitStack() as ctx:
         held = ctx.enter_context(tc.tile_pool(name="held", bufs=1))
-        work = ctx.enter_context(tc.tile_pool(name="work", bufs=4))
+        work = ctx.enter_context(tc.tile_pool(name="work", bufs=M_TILES))
         psum = ctx.enter_context(tc.psum_pool(name="psum", bufs=1))
 
         def keep(name, shape, dtype):
             return held.tile(shape, dtype, name=name, align_bytes=64)
 
-        offs_t = keep("offs_t", [P, S // 16], U16)
-        offs2_t = keep("offs2_t", [P, S2 // 16], U16)
-        pos1_t = keep("pos1_t", [P, PAIRS // 16], U16)
-        pos2_t = keep("pos2_t", [P, PAIRS // 16], U16)
+        def rotating(name, shape, dtype, tag, bufs):
+            return work.tile(shape, dtype, name=name, tag=tag, bufs=bufs, align_bytes=64)
+
+        offs_t = keep("offs_t", [P, S // LIST_COL], U16)
+        offs2_t = keep("offs2_t", [P, S2 // LIST_COL], U16)
+        pos1_t = keep("pos1_t", [P, OUT_COLS // LIST_COL], U16)
+        pos2_t = keep("pos2_t", [P, OUT_COLS // LIST_COL], U16)
         tab_w = keep("tab_w", [P, T], I32)
         tab_s = keep("tab_s", [P, T], U8)
         tab2_w = [keep("tab2_w%d" % g, [P, T2], I32) for g in range(GROUPS)]
         tab2_s = keep("tab2_s", [P, T2], U8)
         w1_raw = [keep("w1_raw%d" % g, [P, PACK, PASS], F32) for g in range(GROUPS)]
-        w4_raw = [keep("w4_raw%d" % g, [P, 2 * PASS], U8) for g in range(GROUPS)]
-        w4_sraw = keep("w4_sraw", [P, H], U8)
-        ref_t = keep("ref_t", [P, M_TILES, PAIRS], F32)
+        w4_raw = keep("w4_raw", [P, 2 * H], U8)
+        w4_raw_s = keep("w4_raw_s", [P, H], U8)
+        ref_t = keep("ref_t", [P, M_TILES, OUT_COLS], F32)
 
-        def load_w1(g, eng):
-            eng.dma_start(w1_raw[g][:], w1[:, g * PASS : (g + 1) * PASS].rearrange("(p i) c -> p i c", i=PACK))
+        def load_w1(g):
+            nc.sync.dma_start(w1_raw[g][:], w1[:, g * PASS : (g + 1) * PASS].rearrange("(p i) c -> p i c", i=PACK))
 
-        def load_w4(g):
-            nc.sync.dma_start(w4_raw[g][:].bitcast(I32), w4_words[0, :, 2 * g * PASS : 2 * (g + 1) * PASS].bitcast(I32))
-
-        def load_plane(eng, plane, rows):
+        def load_plane(plane, rows):
             words = rows.shape[1] // 4
             for quad in range(4):
                 src = rows[4 * quad : 4 * quad + 4, :].bitcast(I32).unsqueeze(0).to_broadcast([8, 4, words])
-                eng.dma_start(plane[32 * quad : 32 * quad + 32, :].bitcast(I32), src)
+                nc.sync.dma_start(plane[32 * quad : 32 * quad + 32, :].bitcast(I32), src)
 
-        if WARM:
-            warm_in = keep("warm_in", [P, 1], F32)
-            warm_out = keep("warm_out", [P, 1], F32)
-            nc.vector.memset(warm_in[:], 1.0)
-            nc.scalar.activation(warm_out[:], warm_in[:], ACT.Abs_reciprocal_sqrt)
+        seed = keep("seed", [P, 1], F32)
+        seed_root = keep("seed_root", [P, 1], F32)
+        one = keep("one", [P, 1], F32)
+        nc.vector.memset(seed[:], 1.0)
+        nc.scalar.activation(seed_root[:], seed[:], ACT.Abs_reciprocal_sqrt)
+        nc.scalar.activation(one[:], seed_root[:], ACT.Sign)
+
         nc.sync.dma_start(offs_t[:], offs)
-        load_plane(nc.sync, tab_s, tab_scales[0])
-        load_w1(0, nc.sync)
+        load_plane(tab_s, tab_scales[0])
+        load_w1(0)
         nc.sync.dma_start(tab_w[:], tab_words[0].rearrange("p t i -> p (t i)").bitcast(I32))
-        load_w4(0)
-        load_plane(nc.sync, w4_sraw, w4_scales[0])
+        nc.sync.dma_start(w4_raw[:].bitcast(I32), w4_words[0].bitcast(I32))
+        load_plane(w4_raw_s, w4_scales[0])
         nc.gpsimd.memset(tab2_s[:].bitcast(I32), 0)
         for g in range(1, GROUPS):
-            load_w1(g, nc.sync)
-            load_w4(g)
+            load_w1(g)
         nc.sync.dma_start(offs2_t[:], offs2)
         for quad in range(4):
             nc.sync.dma_start(
@@ -97,236 +104,229 @@ def tile_list_breath_pattern_response_kernel(
             )
         for g in range(GROUPS):
             nc.sync.dma_start(tab2_w[g][:], tab2_words[g].rearrange("p t i -> p (t i)").bitcast(I32))
-        nc.sync.dma_start(ref_t[:], ref.rearrange("(c p) j -> p c j", p=P))
+        nc.sync.dma_start(ref_t[:], ref.rearrange("(m p) j -> p m j", p=P))
         nc.sync.dma_start(pos1_t[:], pos1)
         nc.sync.dma_start(pos2_t[:], pos2)
 
-        v_w_first = keep("v_w_first", [P, VW], U32)
-        v_w_rest = keep("v_w_rest", [P, S - VW], U32)
-        v_w = [v_w_first[:]] + [v_w_rest[:, c * VW : (c + 1) * VW] for c in range(S // VW - 1)]
-        v_s_all = keep("v_s_all", [P, S], U8)
-        v_s = [v_s_all[:, c * VW : (c + 1) * VW] for c in range(S // VW)]
-        v2_w = [keep("v2_w%d" % g, [P, S2], U32) for g in range(GROUPS)]
-        v2_s = keep("v2_s", [P, S2], U8)
-        w1_bf = [keep("w1_bf%d" % g, [P, PACK * PASS], BF16) for g in range(GROUPS)]
+        v_w_first = keep("v_w_first", [P, PAIR_W], U32)
+        v_w_rest = keep("v_w_rest", [P, S - PAIR_W], U32)
+        v_w = [v_w_first[:]] + [v_w_rest[:, c * PAIR_W : (c + 1) * PAIR_W] for c in range(CHUNKS - 1)]
+        v_s = keep("v_s", [P, S], U8)
         w1_w = [keep("w1_w%d" % g, [P, PASS], U32) for g in range(GROUPS)]
         w1_s = [keep("w1_s%d" % g, [P, PASS], U8) for g in range(GROUPS)]
-        w4_w = [keep("w4_w%d" % g, [P, 2 * PASS], U8) for g in range(GROUPS)]
-        w4_s = [keep("w4_s%d" % g, [P, PASS], U8) for g in range(GROUPS)]
-        h_w_all = [keep("h_w%d" % g, [P, S], U32) for g in range(GROUPS)]
-        h_s_all = [keep("h_s%d" % g, [P, S], U8) for g in range(GROUPS)]
-        h_w = [[h_w_all[g][:, c * VW : (c + 1) * VW] for c in range(S // VW)] for g in range(GROUPS)]
-        h_s = [[h_s_all[g][:, c * VW : (c + 1) * VW] for c in range(S // VW)] for g in range(GROUPS)]
+        w4_w = keep("w4_w", [P, 2 * H], U8)
+        w4_s = keep("w4_s", [P, H], U8)
+        h_w = [keep("h_w%d" % g, [P, S], U32) for g in range(GROUPS)]
+        h_s = [keep("h_s%d" % g, [P, S], U8) for g in range(GROUPS)]
         e_t = [keep("e_t%d" % m, [P, S], F32) for m in range(M_TILES)]
+        made = {}
 
-        def gather_v_words(first):
-            dst, cols = (v_w_first, slice(0, VW // 16)) if first else (v_w_rest, slice(VW // 16, S // 16))
-            nc.vector.tensor_copy(dst[:], tab_w[:].bitcast(U32).indirect(offs_t[:, cols]))
+        def after_pair(pair, name, shape, dtype):
+            return rotating(name, shape, dtype, "after%d" % pair, 1)
 
-        def gather_v_scales():
-            nc.vector.tensor_copy(v_s_all[:], tab_s[:].indirect(offs_t[:]))
+        def gather_v_words(dst, first, last):
+            picks = offs_t[:, first // LIST_COL : last // LIST_COL]
+            nc.vector.tensor_copy(dst[:], tab_w[:].bitcast(U32).indirect(picks))
 
         def gather_v2_words(g):
-            nc.vector.tensor_copy(v2_w[g][:], tab2_w[g][:].bitcast(U32).indirect(offs2_t[:]))
+            made["v2_w", g] = after_pair(V2_AFTER + g, "v2_w", [P, S2], U32)
+            nc.vector.tensor_copy(made["v2_w", g][:], tab2_w[g][:].bitcast(U32).indirect(offs2_t[:]))
 
         def gather_v2_scales():
-            nc.vector.tensor_copy(v2_s[:], tab2_s[:].indirect(offs2_t[:]))
+            made["v2_s", 0] = after_pair(V2_AFTER + GROUPS, "v2_s", [P, S2], U8)
+            nc.vector.tensor_copy(made["v2_s", 0][:], tab2_s[:].indirect(offs2_t[:]))
 
-        def cast_w1(g):
-            dst_all = w1_bf[g][:].rearrange("p (t q i) -> p q i t", t=PACK, i=PACK)
-            src_all = w1_raw[g][:].rearrange("p i (q t) -> p q i t", t=PACK)
-            engines = CAST.split(",")[g]
-            share = P // len(engines)
-            for n, eng in enumerate(engines):
-                dst = dst_all[:, n * share : (n + 1) * share]
-                src = src_all[:, n * share : (n + 1) * share]
-                if eng == "S":
-                    nc.scalar.copy(dst, src)
-                elif eng == "V":
-                    nc.vector.tensor_copy(dst, src)
-                else:
-                    nc.gpsimd.tensor_scalar(dst, src, 1.0, 0.0, ALU.mult, ALU.add)
+        def round_w1(g):
+            if g == GROUPS - 1:
+                rounded = after_pair(CAST_AFTER, "w1_bf", [P, PACK * PASS], BF16)
+            else:
+                rounded = keep("w1_bf%d" % g, [P, PACK * PASS], BF16)
+            made["w1_bf", g] = rounded
+            dst = rounded[:].rearrange("p (t q i) -> p q i t", t=PACK, i=PACK)
+            src = w1_raw[g][:].rearrange("p i (q t) -> p q i t", t=PACK)
+            if g == 0:
+                nc.scalar.copy(dst[:, : P // 2], src[:, : P // 2])
+                nc.vector.tensor_copy(dst[:, P // 2 :], src[:, P // 2 :])
+            else:
+                nc.vector.tensor_copy(dst, src)
 
         def quantise_w1(g):
-            nc.vector.quantize_mx(w1_w[g][:].bitcast(E4M3), w1_s[g][:], w1_bf[g][:])
+            nc.vector.quantize_mx(w1_w[g][:].bitcast(E4M3), w1_s[g][:], made["w1_bf", g][:])
 
-        def deal_w4_words(g):
-            nc.vector.tensor_copy(
-                w4_w[g][:].bitcast(U16).rearrange("p (t o i) -> p o t i", t=PACK, i=8),
-                w4_raw[g][:].bitcast(U16).rearrange("p (o i t) -> p o t i", t=PACK, i=8),
-            )
-
-        def deal_w4_scales(g):
-            nc.vector.tensor_copy(
-                w4_s[g][:].rearrange("p (t o i) -> p o t i", t=PACK, i=16),
-                w4_sraw[:, g * PASS : (g + 1) * PASS].rearrange("p (o i t) -> p o t i", t=PACK, i=16),
-            )
-
-        state = {}
+        def reorder_w4():
+            for dst, src, i_count in ((w4_w[:].bitcast(U16), w4_raw[:].bitcast(U16), 8), (w4_s[:], w4_raw_s[:], 16)):
+                nc.vector.tensor_copy(
+                    dst.rearrange("p (g t o i) -> p o g t i", g=GROUPS, t=PACK, i=i_count),
+                    src.rearrange("p (g o i t) -> p o g t i", g=GROUPS, t=PACK, i=i_count),
+                )
 
         def place(u):
-            pair, half = divmod(u, VW // JW)
-            g, c = ORDER[pair]
-            return g, c, slice(half * JW, (half + 1) * JW)
+            g, c = PAIR_ORDER[u // 2]
+            first = (u % 2) * UNIT_W
+            return g, c, slice(first, first + UNIT_W), slice(c * PAIR_W + first, c * PAIR_W + first + UNIT_W)
+
+        def half(tile, u):
+            return tile[:, (u % 2) * UNIT_W : (u % 2 + 1) * UNIT_W, :]
+
+        def pair_tile(kind, u, dtype, tag, bufs):
+            if u % 2 == 0:
+                made[kind, u // 2] = rotating(kind, [P, PAIR_W, PACK], dtype, tag, bufs)
+            return made[kind, u // 2]
+
+        def chain(n):
+            return "chain%d" % (n % CHAIN), 1
 
         def product_a(u):
-            g, c, cols = place(u)
-            bank = psum.tile([P, PACK, JW], F32, name="a_bank", bufs=3)
+            g, c, in_chunk, curves = place(u)
+            bank = psum.tile([P, PACK, UNIT_W], F32, name="a_bank", bufs=A_BANKS)
             for t in range(PACK):
                 rows = slice(t * P, (t + 1) * P)
                 nc.tensor.matmul_mx(
                     bank[:, t, :], lhsT=w1_w[g][:, rows].bitcast(E4M3), lhsT_scale=w1_s[g][:, rows],
-                    rhs=v_w[c][:, cols].bitcast(E4M3), rhs_scale=v_s[c][:, cols], start=True, stop=True,
+                    rhs=v_w[c][:, in_chunk].bitcast(E4M3), rhs_scale=v_s[:, curves], start=True, stop=True,
                 )
-            state["a", u] = bank
+            made["a", u] = bank
 
         def product_b(u):
-            g, c, cols = place(u)
-            bank = psum.tile([P, PACK, JW], F32, name="b_bank", bufs=3)
+            g, c, in_chunk, curves = place(u)
+            bank = psum.tile([P, PACK, UNIT_W], F32, name="b_bank", bufs=B_BANKS)
             for t in range(PACK):
+                first = g * PASS + t * P
                 nc.tensor.matmul_mx(
-                    bank[:, t, :], lhsT=w4_w[g][:, 2 * t * P : 2 * (t + 1) * P].bitcast(E2M1),
-                    lhsT_scale=w4_s[g][:, t * P : (t + 1) * P],
-                    rhs=v_w[c][:, cols].bitcast(E4M3), rhs_scale=v_s[c][:, cols], start=True, stop=True,
+                    bank[:, t, :], lhsT=w4_w[:, 2 * first : 2 * (first + P)].bitcast(E2M1),
+                    lhsT_scale=w4_s[:, first : first + P],
+                    rhs=v_w[c][:, in_chunk].bitcast(E4M3), rhs_scale=v_s[:, curves], start=True, stop=True,
                 )
-            state["b", u] = bank
-
-        def halves(pair):
-            return (2 * pair, 2 * pair + 1)
-
-        def part(tile, u):
-            return tile[:, (u % 2) * JW : (u % 2 + 1) * JW, :]
-
-        def pair_tile(kind, u, dtype, tag, bufs):
-            if u % 2 == 0:
-                state[kind, u // 2] = work.tile([P, VW, PACK], dtype, name=kind, tag=tag, bufs=bufs, align_bytes=64)
-            return state[kind, u // 2]
+            made["b", u] = bank
 
         def absolute(u):
-            size = pair_tile("size", u, F32, "size", 3)
-            nc.scalar.activation(part(size, u), state["a", u][:].rearrange("p t j -> p j t"), ACT.Abs)
+            size = pair_tile("size", u, F32, *chain(u // 2))
+            nc.scalar.activation(half(size, u), made["a", u][:].rearrange("p t j -> p j t"), ACT.Abs)
 
-        def root(u):
-            r = pair_tile("root", u, F32, "root", 3)
-            size = state["size", u // 2]
-            if u // 2 in FINE:
-                nc.scalar.activation(part(r, u), part(size, u), ACT.Abs_reciprocal_sqrt, bias=1.0)
+        def inverse_root(u):
+            pair = u // 2
+            root = pair_tile("root", u, F32, *(("after%d" % pair, 1) if pair in HELD_ROOTS else ("root", ROOT_BUFS)))
+            size = made["size", pair]
+            if pair in END_PAIRS:
+                nc.scalar.activation(half(root, u), half(size, u), ACT.Abs_reciprocal_sqrt, bias=one[:])
             elif u % 2 == 1:
-                nc.scalar.activation(r[:], size[:], ACT.Abs_reciprocal_sqrt, bias=1.0)
+                nc.scalar.activation(root[:], size[:], ACT.Abs_reciprocal_sqrt, bias=one[:])
 
         def square(u):
-            damp = work.tile([P, JW, PACK], F32, name="damp", tag="ring" if u % 2 else "damp", bufs=3, align_bytes=64)
-            src = part(state["root", u // 2], u)
-            if SQ[u] == "S":
-                nc.scalar.activation(damp[:], src, ACT.Square)
-            elif SQ[u] == "V":
-                nc.vector.tensor_tensor(damp[:], src, src, ALU.mult)
+            pair = u // 2
+            root = half(made["root", pair], u)
+            on_gpsimd = u % 2 == 1 and pair not in END_PAIRS
+            tag, bufs = chain(pair - 1) if on_gpsimd and pair >= 2 else ("damp", DAMP_BUFS)
+            damp = rotating("damp", [P, UNIT_W, PACK], F32, tag, bufs)
+            if on_gpsimd:
+                nc.gpsimd.tensor_tensor(damp[:], root, root, ALU.mult)
+            elif u == 1:
+                nc.vector.tensor_tensor(damp[:], root, root, ALU.mult)
             else:
-                nc.gpsimd.tensor_tensor(damp[:], src, src, ALU.mult)
-            state["damp", u] = damp
+                nc.scalar.activation(damp[:], root, ACT.Square)
+            made["damp", u] = damp
 
         def damped(u):
-            h = pair_tile("h", u, BF16, "ring", 3)
-            nc.vector.tensor_tensor(part(h, u), state["b", u][:].rearrange("p t j -> p j t"), state["damp", u][:], ALU.mult)
+            h = pair_tile("h", u, BF16, *(chain(u // 2 + 1) if u // 2 < CHAINED_H else ("h", PAIRS - CHAINED_H)))
+            nc.vector.tensor_tensor(half(h, u), made["b", u][:].rearrange("p t j -> p j t"), made["damp", u][:], ALU.mult)
 
         def quantise_h(u):
-            g, c, cols = place(u)
-            h = state["h", u // 2]
-            if u // 2 in FINE:
-                nc.vector.quantize_mx(
-                    h_w[g][c][:, cols].bitcast(E4M3), h_s[g][c][:, cols], part(h, u).rearrange("p j t -> p (j t)")
-                )
+            g, c, in_chunk, curves = place(u)
+            h = made["h", u // 2]
+            if u // 2 in END_PAIRS:
+                src = half(h, u)
             elif u % 2 == 1:
-                nc.vector.quantize_mx(h_w[g][c][:].bitcast(E4M3), h_s[g][c][:], h[:].rearrange("p j t -> p (j t)"))
+                src, curves = h[:], slice(c * PAIR_W, (c + 1) * PAIR_W)
+            else:
+                return
+            nc.vector.quantize_mx(h_w[g][:, curves].bitcast(E4M3), h_s[g][:, curves], src.rearrange("p j t -> p (j t)"))
 
-        def score_pass(dst, m, g, c, cols, may_stop=True):
-            cols = slice(c * VW + cols.start, c * VW + cols.stop)
+        def score_pass(dst, m, g, curves, stop):
+            patterns = slice(m * P, (m + 1) * P)
             nc.tensor.matmul_mx(
-                dst, lhsT=v2_w[g][:, m * P : (m + 1) * P].bitcast(E4M3),
-                lhsT_scale=v2_s[4 * g : P, m * P : (m + 1) * P],
-                rhs=h_w_all[g][:, cols].bitcast(E4M3), rhs_scale=h_s_all[g][:, cols],
-                start=(g == 0), stop=(g == GROUPS - 1 and may_stop),
+                dst, lhsT=made["v2_w", g][:, patterns].bitcast(E4M3), lhsT_scale=made["v2_s", 0][4 * g : P, patterns],
+                rhs=h_w[g][:, curves].bitcast(E4M3), rhs_scale=h_s[g][:, curves], start=(g == 0), stop=stop,
             )
 
-        def copy_scores(eng, m, first, src):
-            dst = e_t[m][:, first : first + src.shape[1]]
-            if eng == "S":
-                nc.scalar.copy(dst, src)
-            else:
-                nc.vector.tensor_copy(dst, src)
-
         def scores(u):
-            g, c, cols = place(u)
+            g, c, in_chunk, curves = place(u)
+            chunk = slice(c * PAIR_W, (c + 1) * PAIR_W)
             if u == UNITS - 3:
-                banks = [psum.tile([P, VW], F32, name="e_bank", bufs=2) for m in range(2)]
-                banks = banks + [psum.tile([P, VW], F32, name="a_bank", bufs=3) for m in range(2)]
-                state["last"] = banks
-                for gg in range(GROUPS - 1):
+                banks = [psum.tile([P, PAIR_W], F32, name="e_bank", bufs=E_BANKS) for m in range(E_BANKS)]
+                banks = banks + [psum.tile([P, PAIR_W], F32, name="a_bank", bufs=A_BANKS) for m in range(E_BANKS, M_TILES)]
+                made["last", 0] = banks
+                for earlier in range(GROUPS - 1):
                     for m in range(M_TILES):
-                        score_pass(banks[m][:], m, gg, c, slice(0, VW), False)
+                        score_pass(banks[m][:], m, earlier, chunk, False)
             if g < GROUPS - 1:
                 return
-            if u >= UNITS - 2:
+            if c == CHUNKS - 1:
                 for m in range(M_TILES):
-                    score_pass(state["last"][m][:, cols], m, g, c, cols, u == UNITS - 1)
+                    score_pass(made["last", 0][m][:, in_chunk], m, g, curves, u == UNITS - 1)
                 if u == UNITS - 1:
                     for m in range(M_TILES):
-                        copy_scores("S", m, c * VW, state["last"][m][:])
+                        nc.scalar.copy(e_t[m][:, chunk], made["last", 0][m][:])
             elif c == 1 and u % 2 == 1:
+                both = slice(0, 2 * PAIR_W)
                 for m in range(M_TILES):
-                    bank = psum.tile([P, 2 * VW], F32, name="e_bank", bufs=2)
-                    for gg in range(GROUPS):
-                        score_pass(bank[:], m, gg, 0, slice(0, 2 * VW))
-                    copy_scores(ECOPY[m], m, 0, bank[:])
+                    bank = psum.tile([P, 2 * PAIR_W], F32, name="e_bank", bufs=E_BANKS)
+                    for pass_g in range(GROUPS):
+                        score_pass(bank[:], m, pass_g, both, pass_g == GROUPS - 1)
+                    nc.vector.tensor_copy(e_t[m][:, both], bank[:])
             elif c == 2 and u % 2 == 1:
-                for mm in range(M_TILES // 2):
-                    bank = psum.tile([P, 2, VW], F32, name="e_bank", bufs=2)
+                for m0 in range(0, M_TILES, 2):
+                    bank = psum.tile([P, 2, PAIR_W], F32, name="e_bank", bufs=E_BANKS)
                     for i in range(2):
-                        for gg in range(GROUPS):
-                            score_pass(bank[:, i, :], 2 * mm + i, gg, c, slice(0, VW))
+                        for pass_g in range(GROUPS):
+                            score_pass(bank[:, i, :], m0 + i, pass_g, chunk, pass_g == GROUPS - 1)
                     for i in range(2):
-                        copy_scores(ECOPY[2 * c + mm], 2 * mm + i, c * VW, bank[:, i, :])
+                        nc.scalar.copy(e_t[m0 + i][:, chunk], bank[:, i, :])
 
-        gather_v_scales()
-        cast_w1(0)
+        nc.vector.tensor_copy(v_s[:], tab_s[:].indirect(offs_t[:]))
+        round_w1(0)
         quantise_w1(0)
-        gather_v_words(True)
-        deal_w4_words(0)
-        deal_w4_scales(0)
-        gather_v_words(False)
+        gather_v_words(v_w_first, 0, PAIR_W)
+        gather_v_words(v_w_rest, PAIR_W, S)
+        reorder_w4()
 
-        side = {
-            1: [lambda: cast_w1(1)],
-            3: [lambda: quantise_w1(1), lambda: deal_w4_words(1), lambda: deal_w4_scales(1)],
-            5: [lambda: cast_w1(2)],
-            7: [lambda: quantise_w1(2), lambda: deal_w4_words(2), lambda: deal_w4_scales(2)],
-            11: [gather_v2_scales],
-            13: [lambda: gather_v2_words(0)],
-            15: [lambda: gather_v2_words(1)],
-            17: [lambda: gather_v2_words(2)],
+        stages = [
+            (0, product_a), (ABS_LAG, absolute), (ROOT_LAG, inverse_root), (SQUARE_LAG, square),
+            (B_LAG, product_b), (DAMPED_LAG, damped), (QUANTISE_LAG, quantise_h), (QUANTISE_LAG, scores),
+        ]
+
+        def squares_done(pair):
+            return 2 * pair + 1 + SQUARE_LAG
+
+        beside = {
+            ROOT_LAG: lambda: round_w1(1),
+            SQUARE_LAG: lambda: quantise_w1(1),
+            squares_done(CAST_AFTER): lambda: round_w1(2),
+            squares_done(CAST_AFTER) + 1: lambda: quantise_w1(2),
+            squares_done(V2_AFTER): lambda: gather_v2_words(0),
+            squares_done(V2_AFTER + 1): lambda: gather_v2_words(1),
+            squares_done(V2_AFTER + 2): lambda: gather_v2_words(2),
+            squares_done(V2_AFTER + 3): gather_v2_scales,
         }
-        stages = [(0, product_a), (1, absolute), (2, root), (4, square), (5, product_b), (6, damped), (7, quantise_h), (7, scores)]
-        for step in range(UNITS + 7):
+        for step in range(UNITS + QUANTISE_LAG):
             for lag, stage in stages:
                 if 0 <= step - lag < UNITS:
                     stage(step - lag)
-            for job in side.get(step - 1, []):
-                job()
+            if step in beside:
+                beside[step]()
 
         def less_ref(m):
-            x = work.tile([P, PAIRS], F32, name="x")
+            x = work.tile([P, OUT_COLS], F32, name="x")
             nc.vector.tensor_tensor(x[:], e_t[m][:].indirect(pos1_t[:]), ref_t[:, m, :], ALU.subtract)
-            state["x", m] = x
+            made["x", m] = x
 
         def finish(m):
-            before = work.tile([P, PAIRS], F32, name="before")
-            nc.scalar.activation(before[:], state["x", m][:], ACT.Gelu_apprx_tanh)
-            res = work.tile([P, PAIRS], F32, name="res")
-            pieces = 2 if m == M_TILES - 1 else 1
-            width = PAIRS // pieces
-            for n in range(pieces):
-                cols = slice(n * width, (n + 1) * width)
-                picks = pos2_t[:, cols.start // 16 : cols.stop // 16]
+            before = work.tile([P, OUT_COLS], F32, name="before")
+            nc.scalar.activation(before[:], made["x", m][:], ACT.Gelu_apprx_tanh)
+            res = work.tile([P, OUT_COLS], F32, name="res")
+            width = OUT_COLS // 2 if m == M_TILES - 1 else OUT_COLS
+            for first in range(0, OUT_COLS, width):
+                cols = slice(first, first + width)
+                picks = pos2_t[:, first // LIST_COL : (first + width) // LIST_COL]
                 nc.vector.tensor_tensor(res[:, cols], e_t[m][:].indirect(picks), before[:, cols], ALU.add)
                 nc.sync.dma_start(out[m * P : (m + 1) * P, cols], res[:, cols])
 

from contextlib import ExitStack

import concourse.mybir as mybir

F32 = mybir.dt.float32
BF16 = mybir.dt.bfloat16
I32 = mybir.dt.int32
U32 = mybir.dt.uint32
U16 = mybir.dt.uint16
U8 = mybir.dt.uint8
E4M3 = mybir.dt.float8_e4m3fn_x4
E2M1 = mybir.dt.float4_e2m1fn_x4
ALU = mybir.AluOpType
ACT = mybir.ActivationFunctionType

K, T, S, H, T2, S2, OUT_COLS = 512, 2048, 1024, 1536, 2048, 512, 512
FLOPS = 2 * 2 * K * H * S + 2 * H * S2 * S

P = 128
PACK = 4
PASS = P * PACK
LIST_COL = 16
GROUPS = H // PASS
UNIT_W = 128
PAIR_W = 2 * UNIT_W
CHUNKS = S // PAIR_W
M_TILES = S2 // P

PAIR_ORDER = [(0, c) for c in range(CHUNKS)] + [(g, c) for c in range(CHUNKS) for g in range(1, GROUPS)]
PAIRS = len(PAIR_ORDER)
UNITS = 2 * PAIRS
END_PAIRS = (0, PAIRS - 1)

CHAIN = 5
CHAINED_H = PAIRS - 3
CAST_AFTER = 1
V2_AFTER = 3
HELD_ROOTS = (CAST_AFTER,) + tuple(range(V2_AFTER, V2_AFTER + GROUPS + 1))

A_BANKS, B_BANKS, E_BANKS = 3, 3, 2
ROOT_BUFS = 3
DAMP_BUFS = 4
ABS_LAG, ROOT_LAG, SQUARE_LAG, B_LAG, DAMPED_LAG, QUANTISE_LAG = 1, 2, 4, 5, 6, 7


def tile_list_breath_pattern_response_kernel(
    tc, tab_words, tab_scales, tab2_words, tab2_scales, w1, w4_words, w4_scales, ref, offs, offs2, pos1, pos2, out
):
    nc = tc.nc
    with ExitStack() as ctx:
        held = ctx.enter_context(tc.tile_pool(name="held", bufs=1))
        work = ctx.enter_context(tc.tile_pool(name="work", bufs=M_TILES))
        psum = ctx.enter_context(tc.psum_pool(name="psum", bufs=1))

        def keep(name, shape, dtype):
            return held.tile(shape, dtype, name=name, align_bytes=64)

        def rotating(name, shape, dtype, tag, bufs):
            return work.tile(shape, dtype, name=name, tag=tag, bufs=bufs, align_bytes=64)

        offs_t = keep("offs_t", [P, S // LIST_COL], U16)
        offs2_t = keep("offs2_t", [P, S2 // LIST_COL], U16)
        pos1_t = keep("pos1_t", [P, OUT_COLS // LIST_COL], U16)
        pos2_t = keep("pos2_t", [P, OUT_COLS // LIST_COL], U16)
        tab_w = keep("tab_w", [P, T], I32)
        tab_s = keep("tab_s", [P, T], U8)
        tab2_w = [keep("tab2_w%d" % g, [P, T2], I32) for g in range(GROUPS)]
        tab2_s = keep("tab2_s", [P, T2], U8)
        w1_raw = [keep("w1_raw%d" % g, [P, PACK, PASS], F32) for g in range(GROUPS)]
        w4_raw = keep("w4_raw", [P, 2 * H], U8)
        w4_raw_s = keep("w4_raw_s", [P, H], U8)
        ref_t = keep("ref_t", [P, M_TILES, OUT_COLS], F32)

        def load_w1(g):
            nc.sync.dma_start(w1_raw[g][:], w1[:, g * PASS : (g + 1) * PASS].rearrange("(p i) c -> p i c", i=PACK))

        def load_plane(plane, rows):
            words = rows.shape[1] // 4
            for quad in range(4):
                src = rows[4 * quad : 4 * quad + 4, :].bitcast(I32).unsqueeze(0).to_broadcast([8, 4, words])
                nc.sync.dma_start(plane[32 * quad : 32 * quad + 32, :].bitcast(I32), src)

        seed = keep("seed", [P, 1], F32)
        seed_root = keep("seed_root", [P, 1], F32)
        one = keep("one", [P, 1], F32)
        nc.vector.memset(seed[:], 1.0)
        nc.scalar.activation(seed_root[:], seed[:], ACT.Abs_reciprocal_sqrt)
        nc.scalar.activation(one[:], seed_root[:], ACT.Sign)

        nc.sync.dma_start(offs_t[:], offs)
        load_plane(tab_s, tab_scales[0])
        load_w1(0)
        nc.sync.dma_start(tab_w[:], tab_words[0].rearrange("p t i -> p (t i)").bitcast(I32))
        nc.sync.dma_start(w4_raw[:].bitcast(I32), w4_words[0].bitcast(I32))
        load_plane(w4_raw_s, w4_scales[0])
        nc.gpsimd.memset(tab2_s[:].bitcast(I32), 0)
        for g in range(1, GROUPS):
            load_w1(g)
        nc.sync.dma_start(offs2_t[:], offs2)
        for quad in range(4):
            nc.sync.dma_start(
                tab2_s[32 * quad : 32 * quad + 4 * GROUPS, :].bitcast(I32),
                tab2_scales[:, 4 * quad : 4 * quad + 4, :].bitcast(I32),
            )
        for g in range(GROUPS):
            nc.sync.dma_start(tab2_w[g][:], tab2_words[g].rearrange("p t i -> p (t i)").bitcast(I32))
        nc.sync.dma_start(ref_t[:], ref.rearrange("(m p) j -> p m j", p=P))
        nc.sync.dma_start(pos1_t[:], pos1)
        nc.sync.dma_start(pos2_t[:], pos2)

        v_w_first = keep("v_w_first", [P, PAIR_W], U32)
        v_w_rest = keep("v_w_rest", [P, S - PAIR_W], U32)
        v_w = [v_w_first[:]] + [v_w_rest[:, c * PAIR_W : (c + 1) * PAIR_W] for c in range(CHUNKS - 1)]
        v_s = keep("v_s", [P, S], U8)
        w1_w = [keep("w1_w%d" % g, [P, PASS], U32) for g in range(GROUPS)]
        w1_s = [keep("w1_s%d" % g, [P, PASS], U8) for g in range(GROUPS)]
        w4_w = keep("w4_w", [P, 2 * H], U8)
        w4_s = keep("w4_s", [P, H], U8)
        h_w = [keep("h_w%d" % g, [P, S], U32) for g in range(GROUPS)]
        h_s = [keep("h_s%d" % g, [P, S], U8) for g in range(GROUPS)]
        e_t = [keep("e_t%d" % m, [P, S], F32) for m in range(M_TILES)]
        made = {}

        def after_pair(pair, name, shape, dtype):
            return rotating(name, shape, dtype, "after%d" % pair, 1)

        def gather_v_words(dst, first, last):
            picks = offs_t[:, first // LIST_COL : last // LIST_COL]
            nc.vector.tensor_copy(dst[:], tab_w[:].bitcast(U32).indirect(picks))

        def gather_v2_words(g):
            made["v2_w", g] = after_pair(V2_AFTER + g, "v2_w", [P, S2], U32)
            nc.vector.tensor_copy(made["v2_w", g][:], tab2_w[g][:].bitcast(U32).indirect(offs2_t[:]))

        def gather_v2_scales():
            made["v2_s", 0] = after_pair(V2_AFTER + GROUPS, "v2_s", [P, S2], U8)
            nc.vector.tensor_copy(made["v2_s", 0][:], tab2_s[:].indirect(offs2_t[:]))

        def round_w1(g):
            if g == GROUPS - 1:
                rounded = after_pair(CAST_AFTER, "w1_bf", [P, PACK * PASS], BF16)
            else:
                rounded = keep("w1_bf%d" % g, [P, PACK * PASS], BF16)
            made["w1_bf", g] = rounded
            dst = rounded[:].rearrange("p (t q i) -> p q i t", t=PACK, i=PACK)
            src = w1_raw[g][:].rearrange("p i (q t) -> p q i t", t=PACK)
            if g == 0:
                nc.scalar.copy(dst[:, : P // 2], src[:, : P // 2])
                nc.vector.tensor_copy(dst[:, P // 2 :], src[:, P // 2 :])
            else:
                nc.vector.tensor_copy(dst, src)

        def quantise_w1(g):
            nc.vector.quantize_mx(w1_w[g][:].bitcast(E4M3), w1_s[g][:], made["w1_bf", g][:])

        def reorder_w4():
            for dst, src, i_count in ((w4_w[:].bitcast(U16), w4_raw[:].bitcast(U16), 8), (w4_s[:], w4_raw_s[:], 16)):
                nc.vector.tensor_copy(
                    dst.rearrange("p (g t o i) -> p o g t i", g=GROUPS, t=PACK, i=i_count),
                    src.rearrange("p (g o i t) -> p o g t i", g=GROUPS, t=PACK, i=i_count),
                )

        def place(u):
            g, c = PAIR_ORDER[u // 2]
            first = (u % 2) * UNIT_W
            return g, c, slice(first, first + UNIT_W), slice(c * PAIR_W + first, c * PAIR_W + first + UNIT_W)

        def half(tile, u):
            return tile[:, (u % 2) * UNIT_W : (u % 2 + 1) * UNIT_W, :]

        def pair_tile(kind, u, dtype, tag, bufs):
            if u % 2 == 0:
                made[kind, u // 2] = rotating(kind, [P, PAIR_W, PACK], dtype, tag, bufs)
            return made[kind, u // 2]

        def chain(n):
            return "chain%d" % (n % CHAIN), 1

        def product_a(u):
            g, c, in_chunk, curves = place(u)
            bank = psum.tile([P, PACK, UNIT_W], F32, name="a_bank", bufs=A_BANKS)
            for t in range(PACK):
                rows = slice(t * P, (t + 1) * P)
                nc.tensor.matmul_mx(
                    bank[:, t, :], lhsT=w1_w[g][:, rows].bitcast(E4M3), lhsT_scale=w1_s[g][:, rows],
                    rhs=v_w[c][:, in_chunk].bitcast(E4M3), rhs_scale=v_s[:, curves], start=True, stop=True,
                )
            made["a", u] = bank

        def product_b(u):
            g, c, in_chunk, curves = place(u)
            bank = psum.tile([P, PACK, UNIT_W], F32, name="b_bank", bufs=B_BANKS)
            for t in range(PACK):
                first = g * PASS + t * P
                nc.tensor.matmul_mx(
                    bank[:, t, :], lhsT=w4_w[:, 2 * first : 2 * (first + P)].bitcast(E2M1),
                    lhsT_scale=w4_s[:, first : first + P],
                    rhs=v_w[c][:, in_chunk].bitcast(E4M3), rhs_scale=v_s[:, curves], start=True, stop=True,
                )
            made["b", u] = bank

        def absolute(u):
            size = pair_tile("size", u, F32, *chain(u // 2))
            nc.scalar.activation(half(size, u), made["a", u][:].rearrange("p t j -> p j t"), ACT.Abs)

        def inverse_root(u):
            pair = u // 2
            root = pair_tile("root", u, F32, *(("after%d" % pair, 1) if pair in HELD_ROOTS else ("root", ROOT_BUFS)))
            size = made["size", pair]
            if pair in END_PAIRS:
                nc.scalar.activation(half(root, u), half(size, u), ACT.Abs_reciprocal_sqrt, bias=one[:])
            elif u % 2 == 1:
                nc.scalar.activation(root[:], size[:], ACT.Abs_reciprocal_sqrt, bias=one[:])

        def square(u):
            pair = u // 2
            root = half(made["root", pair], u)
            on_gpsimd = u % 2 == 1 and pair not in END_PAIRS
            tag, bufs = chain(pair - 1) if on_gpsimd and pair >= 2 else ("damp", DAMP_BUFS)
            damp = rotating("damp", [P, UNIT_W, PACK], F32, tag, bufs)
            if on_gpsimd:
                nc.gpsimd.tensor_tensor(damp[:], root, root, ALU.mult)
            elif u == 1:
                nc.vector.tensor_tensor(damp[:], root, root, ALU.mult)
            else:
                nc.scalar.activation(damp[:], root, ACT.Square)
            made["damp", u] = damp

        def damped(u):
            h = pair_tile("h", u, BF16, *(chain(u // 2 + 1) if u // 2 < CHAINED_H else ("h", PAIRS - CHAINED_H)))
            nc.vector.tensor_tensor(half(h, u), made["b", u][:].rearrange("p t j -> p j t"), made["damp", u][:], ALU.mult)

        def quantise_h(u):
            g, c, in_chunk, curves = place(u)
            h = made["h", u // 2]
            if u // 2 in END_PAIRS:
                src = half(h, u)
            elif u % 2 == 1:
                src, curves = h[:], slice(c * PAIR_W, (c + 1) * PAIR_W)
            else:
                return
            nc.vector.quantize_mx(h_w[g][:, curves].bitcast(E4M3), h_s[g][:, curves], src.rearrange("p j t -> p (j t)"))

        def score_pass(dst, m, g, curves, stop):
            patterns = slice(m * P, (m + 1) * P)
            nc.tensor.matmul_mx(
                dst, lhsT=made["v2_w", g][:, patterns].bitcast(E4M3), lhsT_scale=made["v2_s", 0][4 * g : P, patterns],
                rhs=h_w[g][:, curves].bitcast(E4M3), rhs_scale=h_s[g][:, curves], start=(g == 0), stop=stop,
            )

        def scores(u):
            g, c, in_chunk, curves = place(u)
            chunk = slice(c * PAIR_W, (c + 1) * PAIR_W)
            if u == UNITS - 3:
                banks = [psum.tile([P, PAIR_W], F32, name="e_bank", bufs=E_BANKS) for m in range(E_BANKS)]
                banks = banks + [psum.tile([P, PAIR_W], F32, name="a_bank", bufs=A_BANKS) for m in range(E_BANKS, M_TILES)]
                made["last", 0] = banks
                for earlier in range(GROUPS - 1):
                    for m in range(M_TILES):
                        score_pass(banks[m][:], m, earlier, chunk, False)
            if g < GROUPS - 1:
                return
            if c == CHUNKS - 1:
                for m in range(M_TILES):
                    score_pass(made["last", 0][m][:, in_chunk], m, g, curves, u == UNITS - 1)
                if u == UNITS - 1:
                    for m in range(M_TILES):
                        nc.scalar.copy(e_t[m][:, chunk], made["last", 0][m][:])
            elif c == 1 and u % 2 == 1:
                both = slice(0, 2 * PAIR_W)
                for m in range(M_TILES):
                    bank = psum.tile([P, 2 * PAIR_W], F32, name="e_bank", bufs=E_BANKS)
                    for pass_g in range(GROUPS):
                        score_pass(bank[:], m, pass_g, both, pass_g == GROUPS - 1)
                    nc.vector.tensor_copy(e_t[m][:, both], bank[:])
            elif c == 2 and u % 2 == 1:
                for m0 in range(0, M_TILES, 2):
                    bank = psum.tile([P, 2, PAIR_W], F32, name="e_bank", bufs=E_BANKS)
                    for i in range(2):
                        for pass_g in range(GROUPS):
                            score_pass(bank[:, i, :], m0 + i, pass_g, chunk, pass_g == GROUPS - 1)
                    for i in range(2):
                        nc.scalar.copy(e_t[m0 + i][:, chunk], bank[:, i, :])

        nc.vector.tensor_copy(v_s[:], tab_s[:].indirect(offs_t[:]))
        round_w1(0)
        quantise_w1(0)
        gather_v_words(v_w_first, 0, PAIR_W)
        gather_v_words(v_w_rest, PAIR_W, S)
        reorder_w4()

        stages = [
            (0, product_a), (ABS_LAG, absolute), (ROOT_LAG, inverse_root), (SQUARE_LAG, square),
            (B_LAG, product_b), (DAMPED_LAG, damped), (QUANTISE_LAG, quantise_h), (QUANTISE_LAG, scores),
        ]

        def squares_done(pair):
            return 2 * pair + 1 + SQUARE_LAG

        beside = {
            ROOT_LAG: lambda: round_w1(1),
            SQUARE_LAG: lambda: quantise_w1(1),
            squares_done(CAST_AFTER): lambda: round_w1(2),
            squares_done(CAST_AFTER) + 1: lambda: quantise_w1(2),
            squares_done(V2_AFTER): lambda: gather_v2_words(0),
            squares_done(V2_AFTER + 1): lambda: gather_v2_words(1),
            squares_done(V2_AFTER + 2): lambda: gather_v2_words(2),
            squares_done(V2_AFTER + 3): gather_v2_scales,
        }
        for step in range(UNITS + QUANTISE_LAG):
            for lag, stage in stages:
                if 0 <= step - lag < UNITS:
                    stage(step - lag)
            if step in beside:
                beside[step]()

        def less_ref(m):
            x = work.tile([P, OUT_COLS], F32, name="x")
            nc.vector.tensor_tensor(x[:], e_t[m][:].indirect(pos1_t[:]), ref_t[:, m, :], ALU.subtract)
            made["x", m] = x

        def finish(m):
            before = work.tile([P, OUT_COLS], F32, name="before")
            nc.scalar.activation(before[:], made["x", m][:], ACT.Gelu_apprx_tanh)
            res = work.tile([P, OUT_COLS], F32, name="res")
            width = OUT_COLS // 2 if m == M_TILES - 1 else OUT_COLS
            for first in range(0, OUT_COLS, width):
                cols = slice(first, first + width)
                picks = pos2_t[:, first // LIST_COL : (first + width) // LIST_COL]
                nc.vector.tensor_tensor(res[:, cols], e_t[m][:].indirect(picks), before[:, cols], ALU.add)
                nc.sync.dma_start(out[m * P : (m + 1) * P, cols], res[:, cols])

        ahead = 2
        for m in range(ahead):
            less_ref(m)
        for m in range(M_TILES):
            if m + ahead < M_TILES:
                less_ref(m + ahead)
            finish(m)
